import numpy as np
import ml_dtypes


def mxq(x, axis, fmt="e4m3"):
    dtype, down = {"e4m3": (ml_dtypes.float8_e4m3fn, 7), "e5m2": (ml_dtypes.float8_e5m2, 14)}[fmt]
    v = np.moveaxis(np.asarray(x, np.float32).astype(ml_dtypes.bfloat16).astype(np.float64), axis, -1)
    blocks = v.reshape(v.shape[:-1] + (-1, 32))
    amax = np.abs(blocks).max(-1, keepdims=True)
    byte = np.maximum(np.where(amax > 0, np.frexp(amax)[1] - 1 + 127, 0) - down, 1)
    scale = np.exp2(byte - 127.0)
    codes = (blocks / scale).astype(np.float32).astype(dtype).astype(np.float64)
    return np.moveaxis((codes * scale).reshape(v.shape), -1, axis)


WIDE = False


def mx_kscale(k):
    if not WIDE:
        return np.ones(k)
    levels = np.array([10, -10, 5, -5, 0])
    if k % 512:
        return np.exp2(np.random.permutation(np.resize(levels, k // 32))).repeat(32)
    a = np.empty((k // 512, 16))
    for p in range(k // 512):
        a[p, :8] = np.random.permutation(np.resize(levels, 8))
        for g in range(8):
            far = levels[np.abs(levels - a[p, g]) >= 10]
            a[p, g + 8] = far[np.random.randint(len(far))]
    return np.exp2(a.ravel()).repeat(32)


def f64(x):
    return np.asarray(x).astype(np.float64)


def striped(idx):
    return np.tile(idx.reshape(-1, 16).T, (8, 1)).astype(np.uint16)


def unstriped(offs):
    return offs[:16].T.reshape(-1).astype(np.int64)


def pack_weight(w):
    k, n = w.shape
    w = f64(np.asarray(w, np.float32).astype(ml_dtypes.bfloat16)).reshape(k // 32, 32, n)
    amax = np.abs(w).max(1)
    byte = np.clip(np.where(amax > 0, np.frexp(amax)[1] - 1 + 127 - 7, 1), 1, 254)
    scaled = (w * np.exp2(127.0 - byte)[:, None, :]).reshape(k, n).astype(np.float32)
    words = np.ascontiguousarray(scaled.reshape(k // 512, 128, 4, n).transpose(0, 1, 3, 2)).astype(ml_dtypes.float8_e4m3fn).view(np.uint8)
    return words, np.ascontiguousarray(byte.astype(np.uint8).reshape(k // 512, 16, n))


def unpack_weight(words, scales):
    g, p, n, _ = words.shape
    vals = np.ascontiguousarray(words).view(ml_dtypes.float8_e4m3fn).astype(np.float64) * np.repeat(np.exp2(scales.astype(np.float64) - 127.0), 8, axis=1)[..., None]
    return vals.transpose(0, 1, 3, 2).reshape(g * 512, n)


K, T, S, V, N = 512, 4096, 1024, 512, 256


def setup_inputs():
    n = np.random.standard_normal
    s = mx_kscale(K)[:, None]
    packed_w1 = pack_weight(n((K, N)) / np.sqrt(K) / s)
    packed_w2 = pack_weight(n((K, N)) / np.sqrt(K) / s)
    return {
        "xT": (n((K, T)) * s).astype(np.float32),
        "sT": (n((K, V)) * s).astype(np.float32),
        "w1_words": packed_w1[0],
        "w1_scales": packed_w1[1],
        "w2_words": packed_w2[0],
        "w2_scales": packed_w2[1],
        "offs": striped(np.random.permutation(T)[:S]),
        "par": striped(np.random.randint(0, V, S)),
    }


def reference(xT, sT, w1_words, w1_scales, w2_words, w2_scales, offs, par):
    xq = mxq(f64(xT)[:, unstriped(offs)], 0, "e4m3")
    y = unpack_weight(w1_words, w1_scales).T @ xq
    t = unpack_weight(w2_words, w2_scales).T @ mxq(f64(sT), 0, "e4m3")
    return y + t[:, unstriped(par)]

@@ -1,0 +1,161 @@
+from contextlib import ExitStack
+
+import concourse.mybir as mybir
+
+K, T, S, V, N = 512, 4096, 1024, 512, 256
+FLOPS = 2 * K * N * (S + V)
+
+F32 = mybir.dt.float32
+BF16 = mybir.dt.bfloat16
+I32 = mybir.dt.int32
+U32 = mybir.dt.uint32
+U16 = mybir.dt.uint16
+U8 = mybir.dt.uint8
+FP8X4 = mybir.dt.float8_e4m3fn_x4
+COPY = mybir.ActivationFunctionType.Copy
+ADD = mybir.AluOpType.add
+
+P = 128
+PACK = 4
+HALF = S // 2
+SEG = 256
+SPARE = 8
+LAST_CHUNKS = (1024, 1024, 1024, 512, 256, 256)
+VECTOR_CASTS = (3, 4)
+
+
+def tile_picked_fpn_none_e_kernel(tc, xT, sT, w1_words, w1_scales, w2_words, w2_scales, offs, par, out):
+    nc = tc.nc
+    m_tiles = N // P
+    x_rows = xT.rearrange("(p j) c -> p j c", j=PACK)
+
+    with ExitStack() as ctx:
+        keep = ctx.enter_context(tc.tile_pool(name="keep", bufs=1))
+        psum = ctx.enter_context(tc.psum_pool(name="psum", bufs=8))
+
+        offs_t = keep.tile([P, S // 16], U16, name="offs_t")
+        par_t = keep.tile([P, S // 16], U16, name="par_t")
+        s_raw = keep.tile([P, PACK, V], F32, name="s_raw")
+        w1_codes = keep.tile([P, N], U32, name="w1_codes", align_bytes=64)
+        w2_codes = keep.tile([P, N], U32, name="w2_codes", align_bytes=64)
+        w1_plane = keep.tile([P, N], U8, name="w1_plane", align_bytes=64)
+        s_plane = keep.tile([P, V], U8, name="s_plane", align_bytes=64)
+        x_plane = [keep.tile([P, T], F32, name="x_plane%d" % j) for j in range(PACK)]
+        last_bf16 = keep.tile([P, T], BF16, name="last_bf16")
+
+        def load_words(queue, tile, words):
+            queue.dma_start(out=tile[:].bitcast(I32), in_=words[0].rearrange("p n t -> p (n t)").bitcast(I32))
+
+        def load_scales(queue, plane, first, scales):
+            for q in range(4):
+                queue.dma_start(
+                    out=plane[32 * q + first : 32 * q + first + 4, :N].bitcast(I32),
+                    in_=scales[0, 4 * q : 4 * q + 4, :].bitcast(I32),
+                )
+
+        nc.sync.dma_start(out=s_raw[:], in_=sT.rearrange("(p j) v -> p j v", j=PACK))
+        nc.sync.dma_start(par_t[:], par)
+        load_scales(nc.scalar, s_plane, 4, w2_scales)
+        load_words(nc.scalar, w2_codes, w2_words)
+        for j in range(PACK - 1):
+            nc.sync.dma_start(out=x_plane[j][:], in_=x_rows[:, j, :])
+            if j == 0:
+                nc.sync.dma_start(offs_t[:], offs)
+        chunks = []
+        c0 = 0
+        for width in LAST_CHUNKS:
+            chunks.append(slice(c0, c0 + width))
+            c0 = c0 + width
+        for cols in chunks:
+            nc.sync.dma_start(out=x_plane[PACK - 1][:, cols], in_=x_rows[:, PACK - 1, cols])
+        load_words(nc.sync, w1_codes, w1_words)
+
+        t_sb = [keep.tile([P, V + SPARE], F32, name="t_sb%d" % m) for m in range(m_tiles)]
+        for m in range(m_tiles):
+            nc.gpsimd.memset(t_sb[m][:, V:], 0.0)
+        nc.gpsimd.memset(w1_plane[:].bitcast(I32), 0)
+        load_scales(nc.gpsimd, w1_plane, 0, w1_scales)
+
+        s_codes = keep.tile([P, V], U32, name="s_codes", align_bytes=64)
+        s_half = V // 2
+        s_grouped = [keep.tile([P, s_half, PACK], BF16, name="s_grouped%d" % h, align_bytes=64) for h in range(2)]
+        for h in range(2):
+            dst = s_grouped[h][:].rearrange("p (c i) t -> p c t i", i=4)
+            src = s_raw[:, :, h * s_half : (h + 1) * s_half].rearrange("p t (c i) -> p c t i", i=4)
+            if h == 0:
+                nc.vector.tensor_copy(out=dst, in_=src)
+            else:
+                nc.scalar.copy(out=dst, in_=src)
+        for h in range(2):
+            cols = slice(h * s_half, (h + 1) * s_half)
+            nc.vector.quantize_mx(
+                out=s_codes[:, cols].bitcast(FP8X4),
+                scales=s_plane[:, cols],
+                in_=s_grouped[h][:].rearrange("p c t -> p (c t)"),
+            )
+        for m in range(m_tiles):
+            rows = slice(m * P, (m + 1) * P)
+            acc = psum.tile([P, V], F32, name="acc")
+            nc.tensor.matmul_mx(
+                out=acc[:],
+                lhsT=w2_codes[:, rows].bitcast(FP8X4),
+                lhsT_scale=s_plane[4:P, rows],
+                rhs=s_codes[:].bitcast(FP8X4),
+                rhs_scale=s_plane[:],
+                start=True,
+                stop=True,
+            )
+            nc.scalar.activation(out=t_sb[m][:, :V], in_=acc[:], func=COPY)
+
+        def entries(list_tile, h):
+            return list_tile[:, h * HALF // 16 : (h + 1) * HALF // 16]
+
+        t_picked = [keep.tile([P, S], F32, name="t_picked%d" % m) for m in range(m_tiles)]
+        for m in range(m_tiles):
+            for h in range(2):
+                nc.vector.tensor_copy(
+                    out=t_picked[m][:, h * HALF : (h + 1) * HALF], in_=t_sb[m][:].indirect(entries(par_t, h))
+                )
+
+        x_grouped = [keep.tile([P, HALF, PACK], BF16, name="x_grouped%d" % h, align_bytes=64) for h in range(2)]
+        for j in range(PACK - 1):
+            for h in range(2):
+                nc.vector.tensor_copy(out=x_grouped[h][:, :, j], in_=x_plane[j][:].indirect(entries(offs_t, h)))
+
+        last = PACK - 1
+        for i, cols in enumerate(chunks):
+            if i in VECTOR_CASTS:
+                nc.vector.tensor_copy(out=last_bf16[:, cols], in_=x_plane[last][:, cols])
+            else:
+                nc.scalar.activation(out=last_bf16[:, cols], in_=x_plane[last][:, cols], func=COPY)
+        nc.vector.tensor_copy(out=x_grouped[0][:, :, last], in_=x_plane[last][:].indirect(entries(offs_t, 0)))
+        nc.scalar.activation(out=x_grouped[1][:, :, last], in_=last_bf16[:].indirect(entries(offs_t, 1)), func=COPY)
+
+        segs = S // SEG
+        per_half = HALF // SEG
+        x_codes = [keep.tile([P, SEG], U32, name="x_codes%d" % s, align_bytes=64) for s in range(segs)]
+        x_scales = [keep.tile([P, SEG], U8, name="x_scales%d" % s, align_bytes=64) for s in range(segs)]
+        for s in range(segs):
+            lo = (s % per_half) * SEG
+            nc.vector.quantize_mx(
+                out=x_codes[s][:].bitcast(FP8X4),
+                scales=x_scales[s][:],
+                in_=x_grouped[s // per_half][:, lo : lo + SEG, :].rearrange("p c t -> p (c t)"),
+            )
+        for s in range(segs):
+            cols = slice(s * SEG, (s + 1) * SEG)
+            for m in range(m_tiles):
+                rows = slice(m * P, (m + 1) * P)
+                acc = psum.tile([P, SEG], F32, name="acc")
+                nc.tensor.matmul_mx(
+                    out=acc[:],
+                    lhsT=w1_codes[:, rows].bitcast(FP8X4),
+                    lhsT_scale=w1_plane[:, rows],
+                    rhs=x_codes[s][:].bitcast(FP8X4),
+                    rhs_scale=x_scales[s][:],
+                    start=True,
+                    stop=True,
+                )
+                result = keep.tile([P, SEG], F32, name="result%d_%d" % (s, m))
+                nc.vector.tensor_tensor(out=result[:], in0=acc[:], in1=t_picked[m][:, cols], op=ADD)
+                nc.sync.dma_start(out=out[rows, cols], in_=result[:])

@@ -20,8 +20,8 @@ PACK = 4
 HALF = S // 2
 SEG = 256
 SPARE = 8
-LAST_CHUNKS = (1024, 1024, 1024, 512, 256, 256)
-VECTOR_CASTS = (3, 4)
+LAST_CHUNKS = (1024, 1024, 1024, 768, 256)
+VECTOR_SHARE = (0, 0, 512, 512, 0)
 
 
 def tile_picked_fpn_none_e_kernel(tc, xT, sT, w1_words, w1_scales, w2_words, w2_scales, offs, par, out):
@@ -54,9 +54,9 @@ def tile_picked_fpn_none_e_kernel(tc, xT, sT, w1_words, w1_scales, w2_words, w2_
                 )
 
         nc.sync.dma_start(out=s_raw[:], in_=sT.rearrange("(p j) v -> p j v", j=PACK))
+        load_scales(nc.sync, s_plane, 4, w2_scales)
+        load_words(nc.sync, w2_codes, w2_words)
         nc.sync.dma_start(par_t[:], par)
-        load_scales(nc.scalar, s_plane, 4, w2_scales)
-        load_words(nc.scalar, w2_codes, w2_words)
         for j in range(PACK - 1):
             nc.sync.dma_start(out=x_plane[j][:], in_=x_rows[:, j, :])
             if j == 0:
@@ -118,16 +118,23 @@ def tile_picked_fpn_none_e_kernel(tc, xT, sT, w1_words, w1_scales, w2_words, w2_
                 )
 
         x_grouped = [keep.tile([P, HALF, PACK], BF16, name="x_grouped%d" % h, align_bytes=64) for h in range(2)]
-        for j in range(PACK - 1):
+        x_pair = [keep.tile([P, 2, HALF], F32, name="x_pair%d" % h) for h in range(2)]
+        for j in range(2):
             for h in range(2):
-                nc.vector.tensor_copy(out=x_grouped[h][:, :, j], in_=x_plane[j][:].indirect(entries(offs_t, h)))
+                nc.vector.tensor_copy(out=x_pair[h][:, j, :], in_=x_plane[j][:].indirect(entries(offs_t, h)))
+        for h in range(2):
+            nc.scalar.activation(
+                out=x_grouped[h][:, :, 0:2], in_=x_pair[h][:].rearrange("p t c -> p c t"), func=COPY
+            )
+        for h in (1, 0):
+            nc.vector.tensor_copy(out=x_grouped[h][:, :, 2], in_=x_plane[2][:].indirect(entries(offs_t, h)))
 
         last = PACK - 1
-        for i, cols in enumerate(chunks):
-            if i in VECTOR_CASTS:
-                nc.vector.tensor_copy(out=last_bf16[:, cols], in_=x_plane[last][:, cols])
-            else:
-                nc.scalar.activation(out=last_bf16[:, cols], in_=x_plane[last][:, cols], func=COPY)
+        for cols, share in zip(chunks, VECTOR_SHARE):
+            cut = cols.start + share
+            if share:
+                nc.vector.tensor_copy(out=last_bf16[:, cols.start : cut], in_=x_plane[last][:, cols.start : cut])
+            nc.scalar.activation(out=last_bf16[:, cut : cols.stop], in_=x_plane[last][:, cut : cols.stop], func=COPY)
         nc.vector.tensor_copy(out=x_grouped[0][:, :, last], in_=x_plane[last][:].indirect(entries(offs_t, 0)))
         nc.scalar.activation(out=x_grouped[1][:, :, last], in_=last_bf16[:].indirect(entries(offs_t, 1)), func=COPY)
 

@@ -38,7 +38,8 @@ def tile_picked_fpn_none_e_kernel(tc, xT, sT, w1_words, w1_scales, w2_words, w2_
         s_raw = keep.tile([P, PACK, V], F32, name="s_raw")
         w1_codes = keep.tile([P, N], U32, name="w1_codes", align_bytes=64)
         w2_codes = keep.tile([P, N], U32, name="w2_codes", align_bytes=64)
-        w1_plane = keep.tile([P, N], U8, name="w1_plane", align_bytes=64)
+        segs = S // SEG
+        x_scales = [keep.tile([P, SEG], U8, name="x_scales%d" % s, align_bytes=64) for s in range(segs)]
         s_plane = keep.tile([P, V], U8, name="s_plane", align_bytes=64)
         x_plane = [keep.tile([P, T], F32, name="x_plane%d" % j) for j in range(PACK)]
         last_bf16 = keep.tile([P, T], BF16, name="last_bf16")
@@ -61,6 +62,8 @@ def tile_picked_fpn_none_e_kernel(tc, xT, sT, w1_words, w1_scales, w2_words, w2_
             nc.sync.dma_start(out=x_plane[j][:], in_=x_rows[:, j, :])
             if j == 0:
                 nc.sync.dma_start(offs_t[:], offs)
+            if j == 1:
+                load_scales(nc.sync, x_scales[0], 4, w1_scales)
         chunks = []
         c0 = 0
         for width in LAST_CHUNKS:
@@ -72,9 +75,7 @@ def tile_picked_fpn_none_e_kernel(tc, xT, sT, w1_words, w1_scales, w2_words, w2_
 
         t_sb = [keep.tile([P, V + SPARE], F32, name="t_sb%d" % m) for m in range(m_tiles)]
         for m in range(m_tiles):
-            nc.gpsimd.memset(t_sb[m][:, V:], 0.0)
-        nc.gpsimd.memset(w1_plane[:].bitcast(I32), 0)
-        load_scales(nc.gpsimd, w1_plane, 0, w1_scales)
+            nc.vector.memset(t_sb[m][:, V:], 0.0)
 
         s_codes = keep.tile([P, V], U32, name="s_codes", align_bytes=64)
         s_half = V // 2
@@ -110,12 +111,11 @@ def tile_picked_fpn_none_e_kernel(tc, xT, sT, w1_words, w1_scales, w2_words, w2_
         def entries(list_tile, h):
             return list_tile[:, h * HALF // 16 : (h + 1) * HALF // 16]
 
-        t_picked = [keep.tile([P, S], F32, name="t_picked%d" % m) for m in range(m_tiles)]
+        t_picked = {}
         for m in range(m_tiles):
             for h in range(2):
-                nc.vector.tensor_copy(
-                    out=t_picked[m][:, h * HALF : (h + 1) * HALF], in_=t_sb[m][:].indirect(entries(par_t, h))
-                )
+                t_picked[m, h] = keep.tile([P, HALF], F32, name="t_picked%d_%d" % (m, h), tag="t_picked%d_%d" % (m, h), align_bytes=64)
+                nc.vector.tensor_copy(out=t_picked[m, h][:], in_=t_sb[m][:].indirect(entries(par_t, h)))
 
         x_grouped = [keep.tile([P, HALF, PACK], BF16, name="x_grouped%d" % h, align_bytes=64) for h in range(2)]
         x_pair = [keep.tile([P, 2, HALF], F32, name="x_pair%d" % h) for h in range(2)]
@@ -138,31 +138,42 @@ def tile_picked_fpn_none_e_kernel(tc, xT, sT, w1_words, w1_scales, w2_words, w2_
         nc.vector.tensor_copy(out=x_grouped[0][:, :, last], in_=x_plane[last][:].indirect(entries(offs_t, 0)))
         nc.scalar.activation(out=x_grouped[1][:, :, last], in_=last_bf16[:].indirect(entries(offs_t, 1)), func=COPY)
 
-        segs = S // SEG
         per_half = HALF // SEG
-        x_codes = [keep.tile([P, SEG], U32, name="x_codes%d" % s, align_bytes=64) for s in range(segs)]
-        x_scales = [keep.tile([P, SEG], U8, name="x_scales%d" % s, align_bytes=64) for s in range(segs)]
-        for s in range(segs):
+        x_codes = {}
+
+        def quantise(s, tag):
             lo = (s % per_half) * SEG
+            x_codes[s] = keep.tile([P, SEG], U32, name="x_codes%d" % s, tag=tag, align_bytes=64)
             nc.vector.quantize_mx(
                 out=x_codes[s][:].bitcast(FP8X4),
                 scales=x_scales[s][:],
                 in_=x_grouped[s // per_half][:, lo : lo + SEG, :].rearrange("p c t -> p (c t)"),
             )
-        for s in range(segs):
-            cols = slice(s * SEG, (s + 1) * SEG)
+
+        def finish(s, m):
+            lo = (s % per_half) * SEG
+            rows = slice(m * P, (m + 1) * P)
+            acc = psum.tile([P, SEG], F32, name="acc")
+            nc.tensor.matmul_mx(
+                out=acc[:],
+                lhsT=w1_codes[:, rows].bitcast(FP8X4),
+                lhsT_scale=x_scales[0][4:P, rows],
+                rhs=x_codes[s][:].bitcast(FP8X4),
+                rhs_scale=x_scales[s][:],
+                start=True,
+                stop=True,
+            )
+            result = keep.tile([P, SEG], F32, name="result%d_%d" % (s, m))
+            nc.vector.tensor_tensor(out=result[:], in0=acc[:], in1=t_picked[m, s // per_half][:, lo : lo + SEG], op=ADD)
+            nc.sync.dma_start(out=out[rows, s * SEG : (s + 1) * SEG], in_=result[:])
+
+        for s in range(segs - 1):
+            quantise(s, "x_codes%d" % s)
+        finish(0, 0)
+        finish(0, 1)
+        finish(1, 0)
+        quantise(segs - 1, "t_picked0_0")
+        finish(1, 1)
+        for s in range(2, segs):
             for m in range(m_tiles):
-                rows = slice(m * P, (m + 1) * P)
-                acc = psum.tile([P, SEG], F32, name="acc")
-                nc.tensor.matmul_mx(
-                    out=acc[:],
-                    lhsT=w1_codes[:, rows].bitcast(FP8X4),
-                    lhsT_scale=w1_plane[:, rows],
-                    rhs=x_codes[s][:].bitcast(FP8X4),
-                    rhs_scale=x_scales[s][:],
-                    start=True,
-                    stop=True,
-                )
-                result = keep.tile([P, SEG], F32, name="result%d_%d" % (s, m))
-                nc.vector.tensor_tensor(out=result[:], in0=acc[:], in1=t_picked[m][:, cols], op=ADD)
-                nc.sync.dma_start(out=out[rows, cols], in_=result[:])
+                finish(s, m)

@@ -20,8 +20,8 @@ PACK = 4
 HALF = S // 2
 SEG = 256
 SPARE = 8
-LAST_CHUNKS = (1024, 1024, 1024, 768, 256)
-VECTOR_SHARE = (0, 0, 512, 512, 0)
+LAST_CHUNKS = (1024, 1024, 1280, 512, 256)
+VECTOR_SHARE = (0, 0, 768, 256, 0)
 
 
 def tile_picked_fpn_none_e_kernel(tc, xT, sT, w1_words, w1_scales, w2_words, w2_scales, offs, par, out):
@@ -150,29 +150,37 @@ def tile_picked_fpn_none_e_kernel(tc, xT, sT, w1_words, w1_scales, w2_words, w2_
                 in_=x_grouped[s // per_half][:, lo : lo + SEG, :].rearrange("p c t -> p (c t)"),
             )
 
+        accs = {}
+
+        def multiply(s):
+            for m in range(m_tiles):
+                rows = slice(m * P, (m + 1) * P)
+                accs[s, m] = psum.tile([P, SEG], F32, name="acc")
+                nc.tensor.matmul_mx(
+                    out=accs[s, m][:],
+                    lhsT=w1_codes[:, rows].bitcast(FP8X4),
+                    lhsT_scale=x_scales[0][4:P, rows],
+                    rhs=x_codes[s][:].bitcast(FP8X4),
+                    rhs_scale=x_scales[s][:],
+                    start=True,
+                    stop=True,
+                )
+
         def finish(s, m):
             lo = (s % per_half) * SEG
             rows = slice(m * P, (m + 1) * P)
-            acc = psum.tile([P, SEG], F32, name="acc")
-            nc.tensor.matmul_mx(
-                out=acc[:],
-                lhsT=w1_codes[:, rows].bitcast(FP8X4),
-                lhsT_scale=x_scales[0][4:P, rows],
-                rhs=x_codes[s][:].bitcast(FP8X4),
-                rhs_scale=x_scales[s][:],
-                start=True,
-                stop=True,
-            )
             result = keep.tile([P, SEG], F32, name="result%d_%d" % (s, m))
-            nc.vector.tensor_tensor(out=result[:], in0=acc[:], in1=t_picked[m, s // per_half][:, lo : lo + SEG], op=ADD)
+            nc.vector.tensor_tensor(out=result[:], in0=accs[s, m][:], in1=t_picked[m, s // per_half][:, lo : lo + SEG], op=ADD)
             nc.sync.dma_start(out=out[rows, s * SEG : (s + 1) * SEG], in_=result[:])
 
         for s in range(segs - 1):
             quantise(s, "x_codes%d" % s)
+            multiply(s)
         finish(0, 0)
         finish(0, 1)
         finish(1, 0)
-        quantise(segs - 1, "t_picked0_0")
+        quantise(segs - 1, "x_codes1")
+        multiply(segs - 1)
         finish(1, 1)
         for s in range(2, segs):
             for m in range(m_tiles):

@@ -173,14 +173,16 @@ def tile_picked_fpn_none_e_kernel(tc, xT, sT, w1_words, w1_scales, w2_words, w2_
             nc.vector.tensor_tensor(out=result[:], in0=accs[s, m][:], in1=t_picked[m, s // per_half][:, lo : lo + SEG], op=ADD)
             nc.sync.dma_start(out=out[rows, s * SEG : (s + 1) * SEG], in_=result[:])
 
-        for s in range(segs - 1):
+        for s in range(per_half):
             quantise(s, "x_codes%d" % s)
             multiply(s)
         finish(0, 0)
         finish(0, 1)
+        quantise(2, "x_codes0")
+        multiply(2)
         finish(1, 0)
-        quantise(segs - 1, "x_codes1")
-        multiply(segs - 1)
+        quantise(3, "x_codes1")
+        multiply(3)
         finish(1, 1)
         for s in range(2, segs):
             for m in range(m_tiles):

@@ -20,8 +20,8 @@ PACK = 4
 HALF = S // 2
 SEG = 256
 SPARE = 8
-LAST_CHUNKS = (1024, 1024, 1280, 512, 256)
-VECTOR_SHARE = (0, 0, 768, 256, 0)
+LAST_CHUNKS = (1024, 1280, 1152, 512, 128)
+VECTOR_SHARE = (0, 256, 768, 320, 128)
 
 
 def tile_picked_fpn_none_e_kernel(tc, xT, sT, w1_words, w1_scales, w2_words, w2_scales, offs, par, out):
@@ -62,8 +62,6 @@ def tile_picked_fpn_none_e_kernel(tc, xT, sT, w1_words, w1_scales, w2_words, w2_
             nc.sync.dma_start(out=x_plane[j][:], in_=x_rows[:, j, :])
             if j == 0:
                 nc.sync.dma_start(offs_t[:], offs)
-            if j == 1:
-                load_scales(nc.sync, x_scales[0], 4, w1_scales)
         chunks = []
         c0 = 0
         for width in LAST_CHUNKS:
@@ -71,7 +69,6 @@ def tile_picked_fpn_none_e_kernel(tc, xT, sT, w1_words, w1_scales, w2_words, w2_
             c0 = c0 + width
         for cols in chunks:
             nc.sync.dma_start(out=x_plane[PACK - 1][:, cols], in_=x_rows[:, PACK - 1, cols])
-        load_words(nc.sync, w1_codes, w1_words)
 
         t_sb = [keep.tile([P, V + SPARE], F32, name="t_sb%d" % m) for m in range(m_tiles)]
         for m in range(m_tiles):
@@ -108,6 +105,9 @@ def tile_picked_fpn_none_e_kernel(tc, xT, sT, w1_words, w1_scales, w2_words, w2_
             )
             nc.scalar.activation(out=t_sb[m][:, :V], in_=acc[:], func=COPY)
 
+        load_scales(nc.sync, s_plane, 8, w1_scales)
+        load_words(nc.sync, w1_codes, w1_words)
+
         def entries(list_tile, h):
             return list_tile[:, h * HALF // 16 : (h + 1) * HALF // 16]
 
@@ -134,55 +134,66 @@ def tile_picked_fpn_none_e_kernel(tc, xT, sT, w1_words, w1_scales, w2_words, w2_
             cut = cols.start + share
             if share:
                 nc.vector.tensor_copy(out=last_bf16[:, cols.start : cut], in_=x_plane[last][:, cols.start : cut])
-            nc.scalar.activation(out=last_bf16[:, cut : cols.stop], in_=x_plane[last][:, cut : cols.stop], func=COPY)
+            if cut < cols.stop:
+                nc.scalar.activation(out=last_bf16[:, cut : cols.stop], in_=x_plane[last][:, cut : cols.stop], func=COPY)
         nc.vector.tensor_copy(out=x_grouped[0][:, :, last], in_=x_plane[last][:].indirect(entries(offs_t, 0)))
         nc.scalar.activation(out=x_grouped[1][:, :, last], in_=last_bf16[:].indirect(entries(offs_t, 1)), func=COPY)
 
         per_half = HALF // SEG
         x_codes = {}
 
-        def quantise(s, tag):
-            lo = (s % per_half) * SEG
+        def new_codes(s, tag):
             x_codes[s] = keep.tile([P, SEG], U32, name="x_codes%d" % s, tag=tag, align_bytes=64)
+
+        def quantise(s, a=0, b=SEG):
+            lo = (s % per_half) * SEG
             nc.vector.quantize_mx(
-                out=x_codes[s][:].bitcast(FP8X4),
-                scales=x_scales[s][:],
-                in_=x_grouped[s // per_half][:, lo : lo + SEG, :].rearrange("p c t -> p (c t)"),
+                out=x_codes[s][:, a:b].bitcast(FP8X4),
+                scales=x_scales[s][:, a:b],
+                in_=x_grouped[s // per_half][:, lo + a : lo + b, :].rearrange("p c t -> p (c t)"),
+            )
+
+        def multiply(acc, s, m, a=0, b=SEG):
+            rows = slice(m * P, (m + 1) * P)
+            nc.tensor.matmul_mx(
+                out=acc,
+                lhsT=w1_codes[:, rows].bitcast(FP8X4),
+                lhsT_scale=s_plane[8:P, rows],
+                rhs=x_codes[s][:, a:b].bitcast(FP8X4),
+                rhs_scale=x_scales[s][:, a:b],
+                start=True,
+                stop=True,
             )
 
         accs = {}
 
-        def multiply(s):
+        def multiply_both(s):
             for m in range(m_tiles):
-                rows = slice(m * P, (m + 1) * P)
                 accs[s, m] = psum.tile([P, SEG], F32, name="acc")
-                nc.tensor.matmul_mx(
-                    out=accs[s, m][:],
-                    lhsT=w1_codes[:, rows].bitcast(FP8X4),
-                    lhsT_scale=x_scales[0][4:P, rows],
-                    rhs=x_codes[s][:].bitcast(FP8X4),
-                    rhs_scale=x_scales[s][:],
-                    start=True,
-                    stop=True,
-                )
+                multiply(accs[s, m][:], s, m)
+
+        def add(result, acc, s, m, a=0, b=SEG):
+            lo = (s % per_half) * SEG
+            nc.vector.tensor_tensor(out=result, in0=acc, in1=t_picked[m, s // per_half][:, lo + a : lo + b], op=ADD)
+
+        def store(result, s, m):
+            nc.sync.dma_start(out=out[m * P : (m + 1) * P, s * SEG : (s + 1) * SEG], in_=result[:])
 
         def finish(s, m):
-            lo = (s % per_half) * SEG
-            rows = slice(m * P, (m + 1) * P)
             result = keep.tile([P, SEG], F32, name="result%d_%d" % (s, m))
-            nc.vector.tensor_tensor(out=result[:], in0=accs[s, m][:], in1=t_picked[m, s // per_half][:, lo : lo + SEG], op=ADD)
-            nc.sync.dma_start(out=out[rows, s * SEG : (s + 1) * SEG], in_=result[:])
+            add(result[:], accs[s, m][:], s, m)
+            store(result, s, m)
 
-        for s in range(per_half):
-            quantise(s, "x_codes%d" % s)
-            multiply(s)
+        for s in range(segs - 1):
+            new_codes(s, "x_codes%d" % s)
+            quantise(s)
+            multiply_both(s)
         finish(0, 0)
         finish(0, 1)
-        quantise(2, "x_codes0")
-        multiply(2)
         finish(1, 0)
-        quantise(3, "x_codes1")
-        multiply(3)
+        new_codes(3, "x_codes1")
+        quantise(3)
+        multiply_both(3)
         finish(1, 1)
         for s in range(2, segs):
             for m in range(m_tiles):

@@ -21,6 +21,7 @@ HALF = S // 2
 SEG = 256
 SPARE = 8
 LAST_CHUNKS = (1024, 1280, 1152, 512, 128)
+STORE_WIDTHS = (256, 384, 384)
 VECTOR_SHARE = (0, 256, 768, 320, 128)
 
 
@@ -111,11 +112,10 @@ def tile_picked_fpn_none_e_kernel(tc, xT, sT, w1_words, w1_scales, w2_words, w2_
         def entries(list_tile, h):
             return list_tile[:, h * HALF // 16 : (h + 1) * HALF // 16]
 
-        t_picked = {}
+        t_picked = [keep.tile([P, S], F32, name="t_picked%d" % m) for m in range(m_tiles)]
         for m in range(m_tiles):
             for h in range(2):
-                t_picked[m, h] = keep.tile([P, HALF], F32, name="t_picked%d_%d" % (m, h), tag="t_picked%d_%d" % (m, h), align_bytes=64)
-                nc.vector.tensor_copy(out=t_picked[m, h][:], in_=t_sb[m][:].indirect(entries(par_t, h)))
+                nc.vector.tensor_copy(out=t_picked[m][:, h * HALF : (h + 1) * HALF], in_=t_sb[m][:].indirect(entries(par_t, h)))
 
         x_grouped = [keep.tile([P, HALF, PACK], BF16, name="x_grouped%d" % h, align_bytes=64) for h in range(2)]
         x_pair = [keep.tile([P, 2, HALF], F32, name="x_pair%d" % h) for h in range(2)]
@@ -140,61 +140,35 @@ def tile_picked_fpn_none_e_kernel(tc, xT, sT, w1_words, w1_scales, w2_words, w2_
         nc.scalar.activation(out=x_grouped[1][:, :, last], in_=last_bf16[:].indirect(entries(offs_t, 1)), func=COPY)
 
         per_half = HALF // SEG
-        x_codes = {}
-
-        def new_codes(s, tag):
-            x_codes[s] = keep.tile([P, SEG], U32, name="x_codes%d" % s, tag=tag, align_bytes=64)
-
-        def quantise(s, a=0, b=SEG):
+        x_codes = [keep.tile([P, SEG], U32, name="x_codes%d" % s, align_bytes=64) for s in range(segs)]
+        for s in range(segs):
             lo = (s % per_half) * SEG
             nc.vector.quantize_mx(
-                out=x_codes[s][:, a:b].bitcast(FP8X4),
-                scales=x_scales[s][:, a:b],
-                in_=x_grouped[s // per_half][:, lo + a : lo + b, :].rearrange("p c t -> p (c t)"),
+                out=x_codes[s][:].bitcast(FP8X4),
+                scales=x_scales[s][:],
+                in_=x_grouped[s // per_half][:, lo : lo + SEG, :].rearrange("p c t -> p (c t)"),
             )
 
-        def multiply(acc, s, m, a=0, b=SEG):
-            rows = slice(m * P, (m + 1) * P)
-            nc.tensor.matmul_mx(
-                out=acc,
-                lhsT=w1_codes[:, rows].bitcast(FP8X4),
-                lhsT_scale=s_plane[8:P, rows],
-                rhs=x_codes[s][:, a:b].bitcast(FP8X4),
-                rhs_scale=x_scales[s][:, a:b],
-                start=True,
-                stop=True,
-            )
-
-        accs = {}
-
-        def multiply_both(s):
+        first = 0
+        for width in STORE_WIDTHS:
             for m in range(m_tiles):
-                accs[s, m] = psum.tile([P, SEG], F32, name="acc")
-                multiply(accs[s, m][:], s, m)
-
-        def add(result, acc, s, m, a=0, b=SEG):
-            lo = (s % per_half) * SEG
-            nc.vector.tensor_tensor(out=result, in0=acc, in1=t_picked[m, s // per_half][:, lo + a : lo + b], op=ADD)
-
-        def store(result, s, m):
-            nc.sync.dma_start(out=out[m * P : (m + 1) * P, s * SEG : (s + 1) * SEG], in_=result[:])
-
-        def finish(s, m):
-            result = keep.tile([P, SEG], F32, name="result%d_%d" % (s, m))
-            add(result[:], accs[s, m][:], s, m)
-            store(result, s, m)
-
-        for s in range(segs - 1):
-            new_codes(s, "x_codes%d" % s)
-            quantise(s)
-            multiply_both(s)
-        finish(0, 0)
-        finish(0, 1)
-        finish(1, 0)
-        new_codes(3, "x_codes1")
-        quantise(3)
-        multiply_both(3)
-        finish(1, 1)
-        for s in range(2, segs):
-            for m in range(m_tiles):
-                finish(s, m)
+                rows = slice(m * P, (m + 1) * P)
+                acc = psum.tile([P, V], F32, name="acc")
+                a = first
+                while a < first + width:
+                    s = a // SEG
+                    b = min((s + 1) * SEG, first + width)
+                    nc.tensor.matmul_mx(
+                        out=acc[:, a - first : b - first],
+                        lhsT=w1_codes[:, rows].bitcast(FP8X4),
+                        lhsT_scale=s_plane[8:P, rows],
+                        rhs=x_codes[s][:, a - s * SEG : b - s * SEG].bitcast(FP8X4),
+                        rhs_scale=x_scales[s][:, a - s * SEG : b - s * SEG],
+                        start=True,
+                        stop=True,
+                    )
+                    a = b
+                result = keep.tile([P, width], F32, name="result%d_%d" % (first, m))
+                nc.vector.tensor_tensor(out=result[:], in0=acc[:, :width], in1=t_picked[m][:, first : first + width], op=ADD)
+                nc.sync.dma_start(out=out[rows, first : first + width], in_=result[:])
+            first = first + width

@@ -143,11 +143,13 @@ def tile_picked_fpn_none_e_kernel(tc, xT, sT, w1_words, w1_scales, w2_words, w2_
         x_codes = [keep.tile([P, SEG], U32, name="x_codes%d" % s, align_bytes=64) for s in range(segs)]
         for s in range(segs):
             lo = (s % per_half) * SEG
-            nc.vector.quantize_mx(
-                out=x_codes[s][:].bitcast(FP8X4),
-                scales=x_scales[s][:],
-                in_=x_grouped[s // per_half][:, lo : lo + SEG, :].rearrange("p c t -> p (c t)"),
-            )
+            step = P if s == 0 else SEG
+            for a in range(0, SEG, step):
+                nc.vector.quantize_mx(
+                    out=x_codes[s][:, a : a + step].bitcast(FP8X4),
+                    scales=x_scales[s][:, a : a + step],
+                    in_=x_grouped[s // per_half][:, lo + a : lo + a + step, :].rearrange("p c t -> p (c t)"),
+                )
 
         first = 0
         for width in STORE_WIDTHS:
@@ -158,6 +160,8 @@ def tile_picked_fpn_none_e_kernel(tc, xT, sT, w1_words, w1_scales, w2_words, w2_
                 while a < first + width:
                     s = a // SEG
                     b = min((s + 1) * SEG, first + width)
+                    if first == 0 and m == 0:
+                        b = a + P
                     nc.tensor.matmul_mx(
                         out=acc[:, a - first : b - first],
                         lhsT=w1_codes[:, rows].bitcast(FP8X4),

@@ -18,10 +18,10 @@ ADD = mybir.AluOpType.add
 P = 128
 PACK = 4
 HALF = S // 2
-SEG = 256
 SPARE = 8
 LAST_CHUNKS = (1024, 1280, 1152, 512, 128)
-STORE_WIDTHS = (256, 384, 384)
+QUANTISE_WIDTHS = (128, 128, 256, 256, 256)
+PIECES = ((0, (128,)), (1, (256,)), (0, (256,)), (0, (256,)), (1, (256, 128)), (0, (128, 256)), (1, (128, 256)))
 VECTOR_SHARE = (0, 256, 768, 320, 128)
 
 
@@ -39,8 +39,6 @@ def tile_picked_fpn_none_e_kernel(tc, xT, sT, w1_words, w1_scales, w2_words, w2_
         s_raw = keep.tile([P, PACK, V], F32, name="s_raw")
         w1_codes = keep.tile([P, N], U32, name="w1_codes", align_bytes=64)
         w2_codes = keep.tile([P, N], U32, name="w2_codes", align_bytes=64)
-        segs = S // SEG
-        x_scales = [keep.tile([P, SEG], U8, name="x_scales%d" % s, align_bytes=64) for s in range(segs)]
         s_plane = keep.tile([P, V], U8, name="s_plane", align_bytes=64)
         x_plane = [keep.tile([P, T], F32, name="x_plane%d" % j) for j in range(PACK)]
         last_bf16 = keep.tile([P, T], BF16, name="last_bf16")
@@ -139,40 +137,37 @@ def tile_picked_fpn_none_e_kernel(tc, xT, sT, w1_words, w1_scales, w2_words, w2_
         nc.vector.tensor_copy(out=x_grouped[0][:, :, last], in_=x_plane[last][:].indirect(entries(offs_t, 0)))
         nc.scalar.activation(out=x_grouped[1][:, :, last], in_=last_bf16[:].indirect(entries(offs_t, 1)), func=COPY)
 
-        per_half = HALF // SEG
-        x_codes = [keep.tile([P, SEG], U32, name="x_codes%d" % s, align_bytes=64) for s in range(segs)]
-        for s in range(segs):
-            lo = (s % per_half) * SEG
-            step = P if s == 0 else SEG
-            for a in range(0, SEG, step):
-                nc.vector.quantize_mx(
-                    out=x_codes[s][:, a : a + step].bitcast(FP8X4),
-                    scales=x_scales[s][:, a : a + step],
-                    in_=x_grouped[s // per_half][:, lo + a : lo + a + step, :].rearrange("p c t -> p (c t)"),
-                )
-
+        x_codes = keep.tile([P, S], U32, name="x_codes", align_bytes=64)
+        x_scales = keep.tile([P, S], U8, name="x_scales", align_bytes=64)
         first = 0
-        for width in STORE_WIDTHS:
-            for m in range(m_tiles):
-                rows = slice(m * P, (m + 1) * P)
-                acc = psum.tile([P, V], F32, name="acc")
-                a = first
-                while a < first + width:
-                    s = a // SEG
-                    b = min((s + 1) * SEG, first + width)
-                    if first == 0 and m == 0:
-                        b = a + P
-                    nc.tensor.matmul_mx(
-                        out=acc[:, a - first : b - first],
-                        lhsT=w1_codes[:, rows].bitcast(FP8X4),
-                        lhsT_scale=s_plane[8:P, rows],
-                        rhs=x_codes[s][:, a - s * SEG : b - s * SEG].bitcast(FP8X4),
-                        rhs_scale=x_scales[s][:, a - s * SEG : b - s * SEG],
-                        start=True,
-                        stop=True,
-                    )
-                    a = b
-                result = keep.tile([P, width], F32, name="result%d_%d" % (first, m))
-                nc.vector.tensor_tensor(out=result[:], in0=acc[:, :width], in1=t_picked[m][:, first : first + width], op=ADD)
-                nc.sync.dma_start(out=out[rows, first : first + width], in_=result[:])
+        for width in QUANTISE_WIDTHS:
+            lo = first % HALF
+            nc.vector.quantize_mx(
+                out=x_codes[:, first : first + width].bitcast(FP8X4),
+                scales=x_scales[:, first : first + width],
+                in_=x_grouped[first // HALF][:, lo : lo + width, :].rearrange("p c t -> p (c t)"),
+            )
             first = first + width
+
+        done = [0] * m_tiles
+        for m, passes in PIECES:
+            rows = slice(m * P, (m + 1) * P)
+            first = done[m]
+            acc = psum.tile([P, V], F32, name="acc")
+            a = first
+            for n in passes:
+                nc.tensor.matmul_mx(
+                    out=acc[:, a - first : a - first + n],
+                    lhsT=w1_codes[:, rows].bitcast(FP8X4),
+                    lhsT_scale=s_plane[8:P, rows],
+                    rhs=x_codes[:, a : a + n].bitcast(FP8X4),
+                    rhs_scale=x_scales[:, a : a + n],
+                    start=True,
+                    stop=True,
+                )
+                a = a + n
+            width = a - first
+            result = keep.tile([P, width], F32, name="result%d_%d" % (first, m))
+            nc.vector.tensor_tensor(out=result[:], in0=acc[:, :width], in1=t_picked[m][:, first:a], op=ADD)
+            nc.sync.dma_start(out=out[rows, first:a], in_=result[:])
+            done[m] = a

@@ -19,10 +19,10 @@ P = 128
 PACK = 4
 HALF = S // 2
 SPARE = 8
-LAST_CHUNKS = (1024, 1280, 1152, 512, 128)
+LAST_CHUNKS = (1024, 1408, 1152, 384, 128)
 QUANTISE_WIDTHS = (128, 128, 256, 256, 256)
 PIECES = ((0, (128,)), (1, (256,)), (0, (256,)), (0, (256,)), (1, (256, 128)), (0, (128, 256)), (1, (128, 256)))
-VECTOR_SHARE = (0, 256, 768, 320, 128)
+VECTOR_SHARE = (0, 512, 768, 256, 128)
 
 
 def tile_picked_fpn_none_e_kernel(tc, xT, sT, w1_words, w1_scales, w2_words, w2_scales, offs, par, out):

@@ -19,10 +19,10 @@ P = 128
 PACK = 4
 HALF = S // 2
 SPARE = 8
-LAST_CHUNKS = (1024, 1408, 1152, 384, 128)
+LAST_CHUNKS = (1536, 1664, 512, 256, 128)
 QUANTISE_WIDTHS = (128, 128, 256, 256, 256)
 PIECES = ((0, (128,)), (1, (256,)), (0, (256,)), (0, (256,)), (1, (256, 128)), (0, (128, 256)), (1, (128, 256)))
-VECTOR_SHARE = (0, 512, 768, 256, 128)
+VECTOR_SHARE = (0, 768, 512, 256, 128)
 
 
 def tile_picked_fpn_none_e_kernel(tc, xT, sT, w1_words, w1_scales, w2_words, w2_scales, offs, par, out):

@@ -21,7 +21,7 @@ HALF = S // 2
 SPARE = 8
 LAST_CHUNKS = (1536, 1664, 512, 256, 128)
 QUANTISE_WIDTHS = (128, 128, 256, 256, 256)
-PIECES = ((0, (128,)), (1, (256,)), (0, (256,)), (0, (256,)), (1, (256, 128)), (0, (128, 256)), (1, (128, 256)))
+PIECES = ((0, (128,)), (1, (128, 128)), (0, (128, 128)), (0, (128, 128)), (1, (128, 128, 128)), (0, (128, 128, 128)), (1, (128, 128, 128)))
 VECTOR_SHARE = (0, 768, 512, 256, 128)
 
 
@@ -93,19 +93,41 @@ def tile_picked_fpn_none_e_kernel(tc, xT, sT, w1_words, w1_scales, w2_words, w2_
         for m in range(m_tiles):
             rows = slice(m * P, (m + 1) * P)
             acc = psum.tile([P, V], F32, name="acc")
-            nc.tensor.matmul_mx(
-                out=acc[:],
-                lhsT=w2_codes[:, rows].bitcast(FP8X4),
-                lhsT_scale=s_plane[4:P, rows],
-                rhs=s_codes[:].bitcast(FP8X4),
-                rhs_scale=s_plane[:],
-                start=True,
-                stop=True,
-            )
+            for h in range(2):
+                cols = slice(h * s_half, (h + 1) * s_half)
+                nc.tensor.matmul_mx(
+                    out=acc[:, cols],
+                    lhsT=w2_codes[:, rows].bitcast(FP8X4),
+                    lhsT_scale=s_plane[4:P, rows],
+                    rhs=s_codes[:, cols].bitcast(FP8X4),
+                    rhs_scale=s_plane[:, cols],
+                    start=True,
+                    stop=True,
+                )
             nc.scalar.activation(out=t_sb[m][:, :V], in_=acc[:], func=COPY)
 
         load_scales(nc.sync, s_plane, 8, w1_scales)
         load_words(nc.sync, w1_codes, w1_words)
+
+        unread = psum.tile([P, V], F32, name="acc")
+        nc.tensor.matmul_mx(
+            out=unread[:],
+            lhsT=w1_codes[:, :P].bitcast(FP8X4),
+            lhsT_scale=s_plane[8:P, :P],
+            rhs=s_codes[:].bitcast(FP8X4),
+            rhs_scale=s_plane[:],
+            start=True,
+            stop=True,
+        )
+        nc.tensor.matmul_mx(
+            out=unread[: P // 2, :],
+            lhsT=s_codes[:, : P // 2].bitcast(FP8X4),
+            lhsT_scale=s_plane[:, : P // 2],
+            rhs=s_codes[:].bitcast(FP8X4),
+            rhs_scale=s_plane[:],
+            start=True,
+            stop=True,
+        )
 
         def entries(list_tile, h):
             return list_tile[:, h * HALF // 16 : (h + 1) * HALF // 16]

@@ -106,14 +106,14 @@ def tile_picked_fpn_none_e_kernel(tc, xT, sT, w1_words, w1_scales, w2_words, w2_
                 )
             nc.scalar.activation(out=t_sb[m][:, :V], in_=acc[:], func=COPY)
 
-        load_scales(nc.sync, s_plane, 8, w1_scales)
         load_words(nc.sync, w1_codes, w1_words)
+        load_scales(nc.sync, s_plane, 8, w1_scales)
 
         unread = psum.tile([P, V], F32, name="acc")
         nc.tensor.matmul_mx(
             out=unread[:],
             lhsT=w1_codes[:, :P].bitcast(FP8X4),
-            lhsT_scale=s_plane[8:P, :P],
+            lhsT_scale=s_plane[:, :P],
             rhs=s_codes[:].bitcast(FP8X4),
             rhs_scale=s_plane[:],
             start=True,

@@ -109,26 +109,6 @@ def tile_picked_fpn_none_e_kernel(tc, xT, sT, w1_words, w1_scales, w2_words, w2_
         load_words(nc.sync, w1_codes, w1_words)
         load_scales(nc.sync, s_plane, 8, w1_scales)
 
-        unread = psum.tile([P, V], F32, name="acc")
-        nc.tensor.matmul_mx(
-            out=unread[:],
-            lhsT=w1_codes[:, :P].bitcast(FP8X4),
-            lhsT_scale=s_plane[:, :P],
-            rhs=s_codes[:].bitcast(FP8X4),
-            rhs_scale=s_plane[:],
-            start=True,
-            stop=True,
-        )
-        nc.tensor.matmul_mx(
-            out=unread[: P // 2, :],
-            lhsT=s_codes[:, : P // 2].bitcast(FP8X4),
-            lhsT_scale=s_plane[:, : P // 2],
-            rhs=s_codes[:].bitcast(FP8X4),
-            rhs_scale=s_plane[:],
-            start=True,
-            stop=True,
-        )
-
         def entries(list_tile, h):
             return list_tile[:, h * HALF // 16 : (h + 1) * HALF // 16]
 

@@ -19,19 +19,21 @@ P = 128
 PACK = 4
 HALF = S // 2
 SPARE = 8
-LAST_CHUNKS = (1536, 1664, 512, 256, 128)
-QUANTISE_WIDTHS = (128, 128, 256, 256, 256)
-PIECES = ((0, (128,)), (1, (128, 128)), (0, (128, 128)), (0, (128, 128)), (1, (128, 128, 128)), (0, (128, 128, 128)), (1, (128, 128, 128)))
-VECTOR_SHARE = (0, 768, 512, 256, 128)
+WIDTHS = (128, 128, 256, 256, 128, 128)
+RING = 3
+CODE_SLOT = (0, 1, 0, 1, 2, 3)
 
 
 def tile_picked_fpn_none_e_kernel(tc, xT, sT, w1_words, w1_scales, w2_words, w2_scales, offs, par, out):
     nc = tc.nc
     m_tiles = N // P
+    last = PACK - 1
     x_rows = xT.rearrange("(p j) c -> p j c", j=PACK)
+    out_rows = out.rearrange("(m p) c -> p m c", p=P)
 
     with ExitStack() as ctx:
         keep = ctx.enter_context(tc.tile_pool(name="keep", bufs=1))
+        ring = ctx.enter_context(tc.tile_pool(name="ring", bufs=RING))
         psum = ctx.enter_context(tc.psum_pool(name="psum", bufs=8))
 
         offs_t = keep.tile([P, S // 16], U16, name="offs_t")
@@ -41,33 +43,25 @@ def tile_picked_fpn_none_e_kernel(tc, xT, sT, w1_words, w1_scales, w2_words, w2_
         w2_codes = keep.tile([P, N], U32, name="w2_codes", align_bytes=64)
         s_plane = keep.tile([P, V], U8, name="s_plane", align_bytes=64)
         x_plane = [keep.tile([P, T], F32, name="x_plane%d" % j) for j in range(PACK)]
-        last_bf16 = keep.tile([P, T], BF16, name="last_bf16")
 
-        def load_words(queue, tile, words):
-            queue.dma_start(out=tile[:].bitcast(I32), in_=words[0].rearrange("p n t -> p (n t)").bitcast(I32))
+        def load_words(tile, words):
+            nc.sync.dma_start(out=tile[:].bitcast(I32), in_=words[0].rearrange("p n t -> p (n t)").bitcast(I32))
 
-        def load_scales(queue, plane, first, scales):
+        def load_scales(first, scales):
             for q in range(4):
-                queue.dma_start(
-                    out=plane[32 * q + first : 32 * q + first + 4, :N].bitcast(I32),
+                nc.sync.dma_start(
+                    out=s_plane[32 * q + first : 32 * q + first + 4, :N].bitcast(I32),
                     in_=scales[0, 4 * q : 4 * q + 4, :].bitcast(I32),
                 )
 
         nc.sync.dma_start(out=s_raw[:], in_=sT.rearrange("(p j) v -> p j v", j=PACK))
-        load_scales(nc.sync, s_plane, 4, w2_scales)
-        load_words(nc.sync, w2_codes, w2_words)
+        load_scales(4, w2_scales)
+        load_words(w2_codes, w2_words)
         nc.sync.dma_start(par_t[:], par)
-        for j in range(PACK - 1):
+        for j in range(PACK):
             nc.sync.dma_start(out=x_plane[j][:], in_=x_rows[:, j, :])
             if j == 0:
                 nc.sync.dma_start(offs_t[:], offs)
-        chunks = []
-        c0 = 0
-        for width in LAST_CHUNKS:
-            chunks.append(slice(c0, c0 + width))
-            c0 = c0 + width
-        for cols in chunks:
-            nc.sync.dma_start(out=x_plane[PACK - 1][:, cols], in_=x_rows[:, PACK - 1, cols])
 
         t_sb = [keep.tile([P, V + SPARE], F32, name="t_sb%d" % m) for m in range(m_tiles)]
         for m in range(m_tiles):
@@ -106,70 +100,130 @@ def tile_picked_fpn_none_e_kernel(tc, xT, sT, w1_words, w1_scales, w2_words, w2_
                 )
             nc.scalar.activation(out=t_sb[m][:, :V], in_=acc[:], func=COPY)
 
-        load_words(nc.sync, w1_codes, w1_words)
-        load_scales(nc.sync, s_plane, 8, w1_scales)
+        load_words(w1_codes, w1_words)
+        load_scales(8, w1_scales)
 
-        def entries(list_tile, h):
-            return list_tile[:, h * HALF // 16 : (h + 1) * HALF // 16]
+        def entries(list_tile, cols):
+            return list_tile[:, cols.start // 16 : cols.stop // 16]
 
-        t_picked = [keep.tile([P, S], F32, name="t_picked%d" % m) for m in range(m_tiles)]
+        def gather(engine, dst, window, cols):
+            src = window[:].indirect(entries(offs_t, cols))
+            if engine == "vector":
+                nc.vector.tensor_copy(out=dst, in_=src)
+            else:
+                nc.scalar.activation(out=dst, in_=src, func=COPY)
+
+        def move(engine, dst, src):
+            if engine == "vector":
+                nc.vector.tensor_copy(out=dst, in_=src)
+            else:
+                nc.scalar.copy(out=dst, in_=src)
+
+        halves = [slice(0, HALF), slice(HALF, S)]
+        owners = ("vector", "scalar")
+        t_picked = keep.tile([P, m_tiles, S], F32, name="t_picked")
         for m in range(m_tiles):
+            for cols in halves:
+                nc.vector.tensor_copy(out=t_picked[:, m, cols], in_=t_sb[m][:].indirect(entries(par_t, cols)))
+
+        pieces = []
+        c0 = 0
+        for width in WIDTHS:
+            pieces.append(slice(c0, c0 + width))
+            c0 = c0 + width
+
+        early = [keep.tile([P, last, HALF], BF16, name="early%d" % h) for h in range(2)]
+        for j in range(last):
             for h in range(2):
-                nc.vector.tensor_copy(out=t_picked[m][:, h * HALF : (h + 1) * HALF], in_=t_sb[m][:].indirect(entries(par_t, h)))
+                gather(owners[h], early[h][:, j, :], x_plane[j], halves[h])
+        grouped = []
+        late_tiles = {0: (0,), 1: (1,), 2: (2, 3), 4: (4, 5)}
+        late = {}
+        fetched = {}
+        for first, group in late_tiles.items():
+            span = slice(pieces[first].start, pieces[group[-1]].stop)
+            tile = keep.tile([P, span.stop - span.start], BF16, name="late%d" % first)
+            fetched[first] = (tile, span)
+            for i in group:
+                late[i] = tile[:, pieces[i].start - span.start : pieces[i].stop - span.start]
+        for i, cols in enumerate(pieces):
+            h = cols.start // HALF
+            grouped.append(keep.tile([P, WIDTHS[i], PACK], BF16, name="grouped%d" % i, align_bytes=64))
+            lo = cols.start % HALF
+            move(owners[h], grouped[i][:, :, :last], early[h][:, :, lo : lo + WIDTHS[i]].rearrange("p t c -> p c t"))
 
-        x_grouped = [keep.tile([P, HALF, PACK], BF16, name="x_grouped%d" % h, align_bytes=64) for h in range(2)]
-        x_pair = [keep.tile([P, 2, HALF], F32, name="x_pair%d" % h) for h in range(2)]
-        for j in range(2):
-            for h in range(2):
-                nc.vector.tensor_copy(out=x_pair[h][:, j, :], in_=x_plane[j][:].indirect(entries(offs_t, h)))
-        for h in range(2):
-            nc.scalar.activation(
-                out=x_grouped[h][:, :, 0:2], in_=x_pair[h][:].rearrange("p t c -> p c t"), func=COPY
-            )
-        for h in (1, 0):
-            nc.vector.tensor_copy(out=x_grouped[h][:, :, 2], in_=x_plane[2][:].indirect(entries(offs_t, h)))
+        def fetch(engine, i):
+            gather(engine, fetched[i][0][:], x_plane[last], fetched[i][1])
 
-        last = PACK - 1
-        for cols, share in zip(chunks, VECTOR_SHARE):
-            cut = cols.start + share
-            if share:
-                nc.vector.tensor_copy(out=last_bf16[:, cols.start : cut], in_=x_plane[last][:, cols.start : cut])
-            if cut < cols.stop:
-                nc.scalar.activation(out=last_bf16[:, cut : cols.stop], in_=x_plane[last][:, cut : cols.stop], func=COPY)
-        nc.vector.tensor_copy(out=x_grouped[0][:, :, last], in_=x_plane[last][:].indirect(entries(offs_t, 0)))
-        nc.scalar.activation(out=x_grouped[1][:, :, last], in_=last_bf16[:].indirect(entries(offs_t, 1)), func=COPY)
+        def lay(i):
+            move(owners[pieces[i].start // HALF], grouped[i][:, :, last], late[i])
 
-        x_codes = keep.tile([P, S], U32, name="x_codes", align_bytes=64)
-        x_scales = keep.tile([P, S], U8, name="x_scales", align_bytes=64)
-        first = 0
-        for width in QUANTISE_WIDTHS:
-            lo = first % HALF
+        def product(i, targets):
+            codes = keep.tile([P, WIDTHS[i]], U32, name="x_codes%d" % i, tag="x_codes%d" % CODE_SLOT[i], align_bytes=64)
+            scales = ring.tile([P, WIDTHS[i]], U8, name="x_scales", align_bytes=64)
             nc.vector.quantize_mx(
-                out=x_codes[:, first : first + width].bitcast(FP8X4),
-                scales=x_scales[:, first : first + width],
-                in_=x_grouped[first // HALF][:, lo : lo + width, :].rearrange("p c t -> p (c t)"),
+                out=codes[:].bitcast(FP8X4),
+                scales=scales[:],
+                in_=grouped[i][:].rearrange("p c t -> p (c t)"),
             )
-            first = first + width
-
-        done = [0] * m_tiles
-        for m, passes in PIECES:
-            rows = slice(m * P, (m + 1) * P)
-            first = done[m]
-            acc = psum.tile([P, V], F32, name="acc")
-            a = first
-            for n in passes:
+            for m in range(m_tiles):
+                rows = slice(m * P, (m + 1) * P)
                 nc.tensor.matmul_mx(
-                    out=acc[:, a - first : a - first + n],
+                    out=targets[m],
                     lhsT=w1_codes[:, rows].bitcast(FP8X4),
                     lhsT_scale=s_plane[8:P, rows],
-                    rhs=x_codes[:, a : a + n].bitcast(FP8X4),
-                    rhs_scale=x_scales[:, a : a + n],
+                    rhs=codes[:].bitcast(FP8X4),
+                    rhs_scale=scales[:],
                     start=True,
                     stop=True,
                 )
-                a = a + n
-            width = a - first
-            result = keep.tile([P, width], F32, name="result%d_%d" % (first, m))
-            nc.vector.tensor_tensor(out=result[:], in0=acc[:, :width], in1=t_picked[m][:, first:a], op=ADD)
-            nc.sync.dma_start(out=out[rows, first:a], in_=result[:])
-            done[m] = a
+
+        def finish_both(acc, cols):
+            width = cols.stop - cols.start
+            result = keep.tile([P, m_tiles, width], F32, name="both%d" % cols.start)
+            nc.vector.tensor_tensor(
+                out=result[:],
+                in0=acc[:, : m_tiles * width].rearrange("p (m c) -> p m c", m=m_tiles),
+                in1=t_picked[:, :, cols],
+                op=ADD,
+            )
+            nc.sync.dma_start(out=out_rows[:, :, cols], in_=result[:])
+
+        def finish_one(acc, m, cols):
+            width = cols.stop - cols.start
+            result = keep.tile([P, width], F32, name="one%d_%d" % (cols.start, m))
+            nc.vector.tensor_tensor(out=result[:], in0=acc[:, :width], in1=t_picked[:, m, cols], op=ADD)
+            nc.sync.dma_start(out=out_rows[:, m, cols], in_=result[:])
+
+        def bank():
+            return psum.tile([P, V], F32, name="acc")
+
+        fetch("vector", 0)
+        fetch("vector", 1)
+        fetch("scalar", 2)
+        fetch("scalar", 4)
+        lay(0)
+        lay(1)
+        acc0 = bank()
+        product(0, [acc0[:, :128], acc0[:, 128:256]])
+        acc1 = bank()
+        product(1, [acc1[:, :128], acc1[:, 128:256]])
+        lay(2)
+        lay(3)
+        lay(4)
+        lay(5)
+        finish_both(acc0, pieces[0])
+        acc2 = [bank(), bank()]
+        product(2, [acc2[0][:, :256], acc2[1][:, :256]])
+        finish_both(acc1, pieces[1])
+        acc3 = [bank(), bank()]
+        product(3, [acc3[0][:, :256], acc3[1][:, :256]])
+        acc4 = [bank(), bank()]
+        product(4, [acc4[0][:, :128], acc4[1][:, :128]])
+        finish_one(acc2[0], 0, pieces[2])
+        product(5, [acc4[0][:, 128:256], acc4[1][:, 128:256]])
+        finish_one(acc2[1], 1, pieces[2])
+        for m in range(m_tiles):
+            finish_one(acc3[m], m, pieces[3])
+        for m in range(m_tiles):
+            finish_one(acc4[m], m, slice(pieces[4].start, pieces[5].stop))

@@ -19,9 +19,10 @@ P = 128
 PACK = 4
 HALF = S // 2
 SPARE = 8
-WIDTHS = (128, 128, 256, 256, 128, 128)
-RING = 3
-CODE_SLOT = (0, 1, 0, 1, 2, 3)
+QUANTISE_WIDTHS = (128, 128, 256, 256, 256)
+PIECES = ((0, (128,)), (1, (128, 128)), (0, (128, 128)), (0, (128, 128)), (1, (128, 128, 128)), (0, (128, 128, 128)), (1, (128, 128, 128)))
+SMALL = 128
+QUARTER = S // 4
 
 
 def tile_picked_fpn_none_e_kernel(tc, xT, sT, w1_words, w1_scales, w2_words, w2_scales, offs, par, out):
@@ -29,11 +30,9 @@ def tile_picked_fpn_none_e_kernel(tc, xT, sT, w1_words, w1_scales, w2_words, w2_
     m_tiles = N // P
     last = PACK - 1
     x_rows = xT.rearrange("(p j) c -> p j c", j=PACK)
-    out_rows = out.rearrange("(m p) c -> p m c", p=P)
 
     with ExitStack() as ctx:
         keep = ctx.enter_context(tc.tile_pool(name="keep", bufs=1))
-        ring = ctx.enter_context(tc.tile_pool(name="ring", bufs=RING))
         psum = ctx.enter_context(tc.psum_pool(name="psum", bufs=8))
 
         offs_t = keep.tile([P, S // 16], U16, name="offs_t")
@@ -126,104 +125,60 @@ def tile_picked_fpn_none_e_kernel(tc, xT, sT, w1_words, w1_scales, w2_words, w2_
             for cols in halves:
                 nc.vector.tensor_copy(out=t_picked[:, m, cols], in_=t_sb[m][:].indirect(entries(par_t, cols)))
 
-        pieces = []
-        c0 = 0
-        for width in WIDTHS:
-            pieces.append(slice(c0, c0 + width))
-            c0 = c0 + width
-
         early = [keep.tile([P, last, HALF], BF16, name="early%d" % h) for h in range(2)]
         for j in range(last):
             for h in range(2):
                 gather(owners[h], early[h][:, j, :], x_plane[j], halves[h])
+        parts = [halves[0], slice(HALF, HALF + QUARTER), slice(HALF + QUARTER, S)]
         grouped = []
-        late_tiles = {0: (0,), 1: (1,), 2: (2, 3), 4: (4, 5)}
-        late = {}
-        fetched = {}
-        for first, group in late_tiles.items():
-            span = slice(pieces[first].start, pieces[group[-1]].stop)
-            tile = keep.tile([P, span.stop - span.start], BF16, name="late%d" % first)
-            fetched[first] = (tile, span)
-            for i in group:
-                late[i] = tile[:, pieces[i].start - span.start : pieces[i].stop - span.start]
-        for i, cols in enumerate(pieces):
+        for i, cols in enumerate(parts):
             h = cols.start // HALF
-            grouped.append(keep.tile([P, WIDTHS[i], PACK], BF16, name="grouped%d" % i, align_bytes=64))
+            width = cols.stop - cols.start
             lo = cols.start % HALF
-            move(owners[h], grouped[i][:, :, :last], early[h][:, :, lo : lo + WIDTHS[i]].rearrange("p t c -> p c t"))
+            grouped.append(keep.tile([P, width, PACK], BF16, name="grouped%d" % i, align_bytes=64))
+            move(owners[h], grouped[i][:, :, :last], early[h][:, :, lo : lo + width].rearrange("p t c -> p c t"))
 
-        def fetch(engine, i):
-            gather(engine, fetched[i][0][:], x_plane[last], fetched[i][1])
+        gather("vector", grouped[0][:, :, last], x_plane[last], parts[0])
+        for i in range(QUARTER // SMALL):
+            late = keep.tile([P, SMALL], BF16, name="late%d" % i)
+            gather("scalar", late[:], x_plane[last], slice(HALF + i * SMALL, HALF + (i + 1) * SMALL))
+            nc.gpsimd.tensor_copy(out=grouped[1][:, i * SMALL : (i + 1) * SMALL, last], in_=late[:])
+        late_own = keep.tile([P, QUARTER], BF16, name="late_own")
+        gather("scalar", late_own[:], x_plane[last], parts[2])
+        move("scalar", grouped[2][:, :, last], late_own[:])
 
-        def lay(i):
-            move(owners[pieces[i].start // HALF], grouped[i][:, :, last], late[i])
-
-        def product(i, targets):
-            codes = keep.tile([P, WIDTHS[i]], U32, name="x_codes%d" % i, tag="x_codes%d" % CODE_SLOT[i], align_bytes=64)
-            scales = ring.tile([P, WIDTHS[i]], U8, name="x_scales", align_bytes=64)
+        x_codes = keep.tile([P, S], U32, name="x_codes", align_bytes=64)
+        x_scales = keep.tile([P, S], U8, name="x_scales", align_bytes=64)
+        first = 0
+        for width in QUANTISE_WIDTHS:
+            i = max(n for n, cols in enumerate(parts) if cols.start <= first)
+            lo = first - parts[i].start
             nc.vector.quantize_mx(
-                out=codes[:].bitcast(FP8X4),
-                scales=scales[:],
-                in_=grouped[i][:].rearrange("p c t -> p (c t)"),
+                out=x_codes[:, first : first + width].bitcast(FP8X4),
+                scales=x_scales[:, first : first + width],
+                in_=grouped[i][:, lo : lo + width, :].rearrange("p c t -> p (c t)"),
             )
-            for m in range(m_tiles):
-                rows = slice(m * P, (m + 1) * P)
+            first = first + width
+
+        done = [0] * m_tiles
+        for m, passes in PIECES:
+            rows = slice(m * P, (m + 1) * P)
+            first = done[m]
+            acc = psum.tile([P, V], F32, name="acc")
+            a = first
+            for n in passes:
                 nc.tensor.matmul_mx(
-                    out=targets[m],
+                    out=acc[:, a - first : a - first + n],
                     lhsT=w1_codes[:, rows].bitcast(FP8X4),
                     lhsT_scale=s_plane[8:P, rows],
-                    rhs=codes[:].bitcast(FP8X4),
-                    rhs_scale=scales[:],
+                    rhs=x_codes[:, a : a + n].bitcast(FP8X4),
+                    rhs_scale=x_scales[:, a : a + n],
                     start=True,
                     stop=True,
                 )
-
-        def finish_both(acc, cols):
-            width = cols.stop - cols.start
-            result = keep.tile([P, m_tiles, width], F32, name="both%d" % cols.start)
-            nc.vector.tensor_tensor(
-                out=result[:],
-                in0=acc[:, : m_tiles * width].rearrange("p (m c) -> p m c", m=m_tiles),
-                in1=t_picked[:, :, cols],
-                op=ADD,
-            )
-            nc.sync.dma_start(out=out_rows[:, :, cols], in_=result[:])
-
-        def finish_one(acc, m, cols):
-            width = cols.stop - cols.start
-            result = keep.tile([P, width], F32, name="one%d_%d" % (cols.start, m))
-            nc.vector.tensor_tensor(out=result[:], in0=acc[:, :width], in1=t_picked[:, m, cols], op=ADD)
-            nc.sync.dma_start(out=out_rows[:, m, cols], in_=result[:])
-
-        def bank():
-            return psum.tile([P, V], F32, name="acc")
-
-        fetch("vector", 0)
-        fetch("vector", 1)
-        fetch("scalar", 2)
-        fetch("scalar", 4)
-        lay(0)
-        lay(1)
-        acc0 = bank()
-        product(0, [acc0[:, :128], acc0[:, 128:256]])
-        acc1 = bank()
-        product(1, [acc1[:, :128], acc1[:, 128:256]])
-        lay(2)
-        lay(3)
-        lay(4)
-        lay(5)
-        finish_both(acc0, pieces[0])
-        acc2 = [bank(), bank()]
-        product(2, [acc2[0][:, :256], acc2[1][:, :256]])
-        finish_both(acc1, pieces[1])
-        acc3 = [bank(), bank()]
-        product(3, [acc3[0][:, :256], acc3[1][:, :256]])
-        acc4 = [bank(), bank()]
-        product(4, [acc4[0][:, :128], acc4[1][:, :128]])
-        finish_one(acc2[0], 0, pieces[2])
-        product(5, [acc4[0][:, 128:256], acc4[1][:, 128:256]])
-        finish_one(acc2[1], 1, pieces[2])
-        for m in range(m_tiles):
-            finish_one(acc3[m], m, pieces[3])
-        for m in range(m_tiles):
-            finish_one(acc4[m], m, slice(pieces[4].start, pieces[5].stop))
+                a = a + n
+            width = a - first
+            result = keep.tile([P, width], F32, name="result%d_%d" % (first, m))
+            nc.vector.tensor_tensor(out=result[:], in0=acc[:, :width], in1=t_picked[:, m, first:a], op=ADD)
+            nc.sync.dma_start(out=out[rows, first:a], in_=result[:])
+            done[m] = a

@@ -19,7 +19,6 @@ P = 128
 PACK = 4
 HALF = S // 2
 SPARE = 8
-QUANTISE_WIDTHS = (128, 128, 256, 256, 256)
 PIECES = ((0, (128,)), (1, (128, 128)), (0, (128, 128)), (0, (128, 128)), (1, (128, 128, 128)), (0, (128, 128, 128)), (1, (128, 128, 128)))
 SMALL = 128
 QUARTER = S // 4
@@ -125,45 +124,61 @@ def tile_picked_fpn_none_e_kernel(tc, xT, sT, w1_words, w1_scales, w2_words, w2_
             for cols in halves:
                 nc.vector.tensor_copy(out=t_picked[:, m, cols], in_=t_sb[m][:].indirect(entries(par_t, cols)))
 
-        early = [keep.tile([P, last, HALF], BF16, name="early%d" % h) for h in range(2)]
+        parts = [slice(0, 128), slice(128, 640), slice(640, 768), slice(768, 1024)]
+        grouped = [
+            keep.tile([P, cols.stop - cols.start, PACK], BF16, name="grouped%d" % i, align_bytes=64)
+            for i, cols in enumerate(parts)
+        ]
+        early_v = keep.tile([P, last, HALF], BF16, name="early_v")
+        early_s = keep.tile([P, last, HALF], BF16, name="early_s")
         for j in range(last):
-            for h in range(2):
-                gather(owners[h], early[h][:, j, :], x_plane[j], halves[h])
-        parts = [halves[0], slice(HALF, HALF + QUARTER), slice(HALF + QUARTER, S)]
-        grouped = []
-        for i, cols in enumerate(parts):
-            h = cols.start // HALF
-            width = cols.stop - cols.start
-            lo = cols.start % HALF
-            grouped.append(keep.tile([P, width, PACK], BF16, name="grouped%d" % i, align_bytes=64))
-            move(owners[h], grouped[i][:, :, :last], early[h][:, :, lo : lo + width].rearrange("p t c -> p c t"))
+            gather("vector", early_v[:, j, :], x_plane[j], parts[1])
+            gather("scalar", early_s[:, j, :SMALL], x_plane[j], parts[0])
+            gather("scalar", early_s[:, j, SMALL:], x_plane[j], slice(parts[2].start, S))
+        move("vector", grouped[1][:, :, :last], early_v[:].rearrange("p t c -> p c t"))
+        lo = 0
+        for i in (0, 2, 3):
+            width = parts[i].stop - parts[i].start
+            move("scalar", grouped[i][:, :, :last], early_s[:, :, lo : lo + width].rearrange("p t c -> p c t"))
+            lo = lo + width
 
-        gather("vector", grouped[0][:, :, last], x_plane[last], parts[0])
-        for i in range(QUARTER // SMALL):
-            late = keep.tile([P, SMALL], BF16, name="late%d" % i)
-            gather("scalar", late[:], x_plane[last], slice(HALF + i * SMALL, HALF + (i + 1) * SMALL))
-            nc.gpsimd.tensor_copy(out=grouped[1][:, i * SMALL : (i + 1) * SMALL, last], in_=late[:])
-        late_own = keep.tile([P, QUARTER], BF16, name="late_own")
-        gather("scalar", late_own[:], x_plane[last], parts[2])
-        move("scalar", grouped[2][:, :, last], late_own[:])
+        gather("vector", grouped[1][:, :, last], x_plane[last], parts[1])
+        for i in (0, 2):
+            late = keep.tile([P, SMALL], BF16, name="late%d" % i, tag="shared%d" % i, align_bytes=64)
+            gather("scalar", late[:], x_plane[last], parts[i])
+            nc.gpsimd.tensor_copy(out=grouped[i][:, :, last], in_=late[:])
+        own = [slice(i * SMALL, (i + 1) * SMALL) for i in range(QUARTER // SMALL)]
+        late_own = [keep.tile([P, SMALL], BF16, name="late_own%d" % i) for i in range(len(own))]
+        for i, cols in enumerate(own):
+            gather("scalar", late_own[i][:], x_plane[last], slice(parts[3].start + cols.start, parts[3].start + cols.stop))
+        for i, cols in enumerate(own):
+            move("scalar", grouped[3][:, cols, last], late_own[i][:])
 
-        x_codes = keep.tile([P, S], U32, name="x_codes", align_bytes=64)
         x_scales = keep.tile([P, S], U8, name="x_scales", align_bytes=64)
-        first = 0
-        for width in QUANTISE_WIDTHS:
-            i = max(n for n, cols in enumerate(parts) if cols.start <= first)
-            lo = first - parts[i].start
-            nc.vector.quantize_mx(
-                out=x_codes[:, first : first + width].bitcast(FP8X4),
-                scales=x_scales[:, first : first + width],
-                in_=grouped[i][:, lo : lo + width, :].rearrange("p c t -> p (c t)"),
-            )
-            first = first + width
+        x_codes = []
 
-        done = [0] * m_tiles
-        for m, passes in PIECES:
+        def quantise(i):
+            cols = parts[i]
+            width = cols.stop - cols.start
+            tag = ("x_codes0", "shared0", "x_codes2", "x_codes0")[i]
+            x_codes.append(keep.tile([P, width], U32, name="x_codes%d" % i, tag=tag, align_bytes=64))
+            for lo in range(0, width, QUARTER):
+                hi = min(lo + QUARTER, width)
+                nc.vector.quantize_mx(
+                    out=x_codes[i][:, lo:hi].bitcast(FP8X4),
+                    scales=x_scales[:, cols.start + lo : cols.start + hi],
+                    in_=grouped[i][:, lo:hi, :].rearrange("p c t -> p (c t)"),
+                )
+
+        for i in range(3):
+            quantise(i)
+
+        def codes_at(a, n):
+            i = max(k for k, cols in enumerate(parts) if cols.start <= a)
+            return x_codes[i][:, a - parts[i].start : a - parts[i].start + n]
+
+        def product(m, first, passes):
             rows = slice(m * P, (m + 1) * P)
-            first = done[m]
             acc = psum.tile([P, V], F32, name="acc")
             a = first
             for n in passes:
@@ -171,14 +186,29 @@ def tile_picked_fpn_none_e_kernel(tc, xT, sT, w1_words, w1_scales, w2_words, w2_
                     out=acc[:, a - first : a - first + n],
                     lhsT=w1_codes[:, rows].bitcast(FP8X4),
                     lhsT_scale=s_plane[8:P, rows],
-                    rhs=x_codes[:, a : a + n].bitcast(FP8X4),
+                    rhs=codes_at(a, n).bitcast(FP8X4),
                     rhs_scale=x_scales[:, a : a + n],
                     start=True,
                     stop=True,
                 )
                 a = a + n
-            width = a - first
+            return acc
+
+        def finish(m, first, width, acc):
             result = keep.tile([P, width], F32, name="result%d_%d" % (first, m))
-            nc.vector.tensor_tensor(out=result[:], in0=acc[:, :width], in1=t_picked[:, m, first:a], op=ADD)
-            nc.sync.dma_start(out=out[rows, first:a], in_=result[:])
-            done[m] = a
+            nc.vector.tensor_tensor(out=result[:], in0=acc[:, :width], in1=t_picked[:, m, first : first + width], op=ADD)
+            nc.sync.dma_start(out=out[m * P : (m + 1) * P, first : first + width], in_=result[:])
+
+        done = [0] * m_tiles
+        starts = []
+        for m, passes in PIECES:
+            starts.append(done[m])
+            done[m] = done[m] + sum(passes)
+        accs = [product(m, starts[i], passes) for i, (m, passes) in enumerate(PIECES[:2])]
+        finish(PIECES[0][0], starts[0], sum(PIECES[0][1]), accs[0])
+        quantise(3)
+        for i, (m, passes) in enumerate(PIECES):
+            if i >= 2:
+                accs.append(product(m, starts[i], passes))
+            if i >= 1:
+                finish(m, starts[i], sum(passes), accs[i])

@@ -40,7 +40,9 @@ def tile_picked_fpn_none_e_kernel(tc, xT, sT, w1_words, w1_scales, w2_words, w2_
         w1_codes = keep.tile([P, N], U32, name="w1_codes", align_bytes=64)
         w2_codes = keep.tile([P, N], U32, name="w2_codes", align_bytes=64)
         s_plane = keep.tile([P, V], U8, name="s_plane", align_bytes=64)
-        x_plane = [keep.tile([P, T], F32, name="x_plane%d" % j) for j in range(PACK)]
+        x_pair = keep.tile([P, 2 * T], F32, name="x_pair")
+        x_single = [keep.tile([P, T], F32, name="x_single%d" % j) for j in range(2)]
+        x_plane = [x_pair[:, :T], x_pair[:, T:], x_single[0][:], x_single[1][:]]
 
         def load_words(tile, words):
             nc.sync.dma_start(out=tile[:].bitcast(I32), in_=words[0].rearrange("p n t -> p (n t)").bitcast(I32))
@@ -56,10 +58,10 @@ def tile_picked_fpn_none_e_kernel(tc, xT, sT, w1_words, w1_scales, w2_words, w2_
         load_scales(4, w2_scales)
         load_words(w2_codes, w2_words)
         nc.sync.dma_start(par_t[:], par)
-        for j in range(PACK):
-            nc.sync.dma_start(out=x_plane[j][:], in_=x_rows[:, j, :])
-            if j == 0:
-                nc.sync.dma_start(offs_t[:], offs)
+        nc.sync.dma_start(out=x_pair[:], in_=xT.rearrange("(p j) c -> p (j c)", j=PACK)[:, : 2 * T])
+        nc.sync.dma_start(offs_t[:], offs)
+        for j in (2, 3):
+            nc.sync.dma_start(out=x_plane[j], in_=x_rows[:, j, :])
 
         t_sb = [keep.tile([P, V + SPARE], F32, name="t_sb%d" % m) for m in range(m_tiles)]
         for m in range(m_tiles):
@@ -105,7 +107,7 @@ def tile_picked_fpn_none_e_kernel(tc, xT, sT, w1_words, w1_scales, w2_words, w2_
             return list_tile[:, cols.start // 16 : cols.stop // 16]
 
         def gather(engine, dst, window, cols):
-            src = window[:].indirect(entries(offs_t, cols))
+            src = window.indirect(entries(offs_t, cols))
             if engine == "vector":
                 nc.vector.tensor_copy(out=dst, in_=src)
             else:
@@ -129,13 +131,11 @@ def tile_picked_fpn_none_e_kernel(tc, xT, sT, w1_words, w1_scales, w2_words, w2_
             keep.tile([P, cols.stop - cols.start, PACK], BF16, name="grouped%d" % i, align_bytes=64)
             for i, cols in enumerate(parts)
         ]
-        early_v = keep.tile([P, last, HALF], BF16, name="early_v")
-        early_s = keep.tile([P, last, HALF], BF16, name="early_s")
+        early_s = keep.tile([P, last, HALF], F32, name="early_s")
         for j in range(last):
-            gather("vector", early_v[:, j, :], x_plane[j], parts[1])
+            gather("vector", grouped[1][:, :, j], x_plane[j], parts[1])
             gather("scalar", early_s[:, j, :SMALL], x_plane[j], parts[0])
             gather("scalar", early_s[:, j, SMALL:], x_plane[j], slice(parts[2].start, S))
-        move("vector", grouped[1][:, :, :last], early_v[:].rearrange("p t c -> p c t"))
         lo = 0
         for i in (0, 2, 3):
             width = parts[i].stop - parts[i].start

from contextlib import ExitStack

import concourse.mybir as mybir

K, T, S, V, N = 512, 4096, 1024, 512, 256
FLOPS = 2 * K * N * (S + V)

F32 = mybir.dt.float32
BF16 = mybir.dt.bfloat16
I32 = mybir.dt.int32
U32 = mybir.dt.uint32
U16 = mybir.dt.uint16
U8 = mybir.dt.uint8
FP8X4 = mybir.dt.float8_e4m3fn_x4
COPY = mybir.ActivationFunctionType.Copy
ADD = mybir.AluOpType.add

P = 128
PACK = 4
HALF = S // 2
SPARE = 8
PIECES = ((0, (128,)), (1, (128, 128)), (0, (128, 128)), (0, (128, 128)), (1, (128, 128, 128)), (0, (128, 128, 128)), (1, (128, 128, 128)))
SMALL = 128
QUARTER = S // 4


def tile_picked_fpn_none_e_kernel(tc, xT, sT, w1_words, w1_scales, w2_words, w2_scales, offs, par, out):
    nc = tc.nc
    m_tiles = N // P
    last = PACK - 1
    x_rows = xT.rearrange("(p j) c -> p j c", j=PACK)

    with ExitStack() as ctx:
        keep = ctx.enter_context(tc.tile_pool(name="keep", bufs=1))
        psum = ctx.enter_context(tc.psum_pool(name="psum", bufs=8))

        offs_t = keep.tile([P, S // 16], U16, name="offs_t")
        par_t = keep.tile([P, S // 16], U16, name="par_t")
        s_raw = keep.tile([P, PACK, V], F32, name="s_raw")
        w1_codes = keep.tile([P, N], U32, name="w1_codes", align_bytes=64)
        w2_codes = keep.tile([P, N], U32, name="w2_codes", align_bytes=64)
        s_plane = keep.tile([P, V], U8, name="s_plane", align_bytes=64)
        x_pair = keep.tile([P, 2 * T], F32, name="x_pair")
        x_single = [keep.tile([P, T], F32, name="x_single%d" % j) for j in range(2)]
        x_plane = [x_pair[:, :T], x_pair[:, T:], x_single[0][:], x_single[1][:]]

        def load_words(tile, words):
            nc.sync.dma_start(out=tile[:].bitcast(I32), in_=words[0].rearrange("p n t -> p (n t)").bitcast(I32))

        def load_scales(first, scales):
            for q in range(4):
                nc.sync.dma_start(
                    out=s_plane[32 * q + first : 32 * q + first + 4, :N].bitcast(I32),
                    in_=scales[0, 4 * q : 4 * q + 4, :].bitcast(I32),
                )

        nc.sync.dma_start(out=s_raw[:], in_=sT.rearrange("(p j) v -> p j v", j=PACK))
        load_scales(4, w2_scales)
        load_words(w2_codes, w2_words)
        nc.sync.dma_start(par_t[:], par)
        nc.sync.dma_start(out=x_pair[:], in_=xT.rearrange("(p j) c -> p (j c)", j=PACK)[:, : 2 * T])
        nc.sync.dma_start(offs_t[:], offs)
        for j in (2, 3):
            nc.sync.dma_start(out=x_plane[j], in_=x_rows[:, j, :])

        t_sb = [keep.tile([P, V + SPARE], F32, name="t_sb%d" % m) for m in range(m_tiles)]
        for m in range(m_tiles):
            nc.vector.memset(t_sb[m][:, V:], 0.0)

        s_codes = keep.tile([P, V], U32, name="s_codes", align_bytes=64)
        s_half = V // 2
        s_grouped = [keep.tile([P, s_half, PACK], BF16, name="s_grouped%d" % h, align_bytes=64) for h in range(2)]
        for h in range(2):
            dst = s_grouped[h][:].rearrange("p (c i) t -> p c t i", i=4)
            src = s_raw[:, :, h * s_half : (h + 1) * s_half].rearrange("p t (c i) -> p c t i", i=4)
            if h == 0:
                nc.vector.tensor_copy(out=dst, in_=src)
            else:
                nc.scalar.copy(out=dst, in_=src)
        for h in range(2):
            cols = slice(h * s_half, (h + 1) * s_half)
            nc.vector.quantize_mx(
                out=s_codes[:, cols].bitcast(FP8X4),
                scales=s_plane[:, cols],
                in_=s_grouped[h][:].rearrange("p c t -> p (c t)"),
            )
        for m in range(m_tiles):
            rows = slice(m * P, (m + 1) * P)
            acc = psum.tile([P, V], F32, name="acc")
            for h in range(2):
                cols = slice(h * s_half, (h + 1) * s_half)
                nc.tensor.matmul_mx(
                    out=acc[:, cols],
                    lhsT=w2_codes[:, rows].bitcast(FP8X4),
                    lhsT_scale=s_plane[4:P, rows],
                    rhs=s_codes[:, cols].bitcast(FP8X4),
                    rhs_scale=s_plane[:, cols],
                    start=True,
                    stop=True,
                )
            nc.scalar.activation(out=t_sb[m][:, :V], in_=acc[:], func=COPY)

        load_words(w1_codes, w1_words)
        load_scales(8, w1_scales)

        def entries(list_tile, cols):
            return list_tile[:, cols.start // 16 : cols.stop // 16]

        def gather(engine, dst, window, cols):
            src = window.indirect(entries(offs_t, cols))
            if engine == "vector":
                nc.vector.tensor_copy(out=dst, in_=src)
            else:
                nc.scalar.activation(out=dst, in_=src, func=COPY)

        def move(engine, dst, src):
            if engine == "vector":
                nc.vector.tensor_copy(out=dst, in_=src)
            else:
                nc.scalar.copy(out=dst, in_=src)

        halves = [slice(0, HALF), slice(HALF, S)]
        owners = ("vector", "scalar")
        t_picked = keep.tile([P, m_tiles, S], F32, name="t_picked")
        for m in range(m_tiles):
            for cols in halves:
                nc.vector.tensor_copy(out=t_picked[:, m, cols], in_=t_sb[m][:].indirect(entries(par_t, cols)))

        parts = [slice(0, 128), slice(128, 640), slice(640, 768), slice(768, 1024)]
        grouped = [
            keep.tile([P, cols.stop - cols.start, PACK], BF16, name="grouped%d" % i, align_bytes=64)
            for i, cols in enumerate(parts)
        ]
        early_s = keep.tile([P, last, HALF], F32, name="early_s")
        for j in range(last):
            gather("vector", grouped[1][:, :, j], x_plane[j], parts[1])
            gather("scalar", early_s[:, j, :SMALL], x_plane[j], parts[0])
            gather("scalar", early_s[:, j, SMALL:], x_plane[j], slice(parts[2].start, S))
        lo = 0
        for i in (0, 2, 3):
            width = parts[i].stop - parts[i].start
            move("scalar", grouped[i][:, :, :last], early_s[:, :, lo : lo + width].rearrange("p t c -> p c t"))
            lo = lo + width

        gather("vector", grouped[1][:, :, last], x_plane[last], parts[1])
        for i in (0, 2):
            late = keep.tile([P, SMALL], BF16, name="late%d" % i, tag="shared%d" % i, align_bytes=64)
            gather("scalar", late[:], x_plane[last], parts[i])
            nc.gpsimd.tensor_copy(out=grouped[i][:, :, last], in_=late[:])
        own = [slice(i * SMALL, (i + 1) * SMALL) for i in range(QUARTER // SMALL)]
        late_own = [keep.tile([P, SMALL], BF16, name="late_own%d" % i) for i in range(len(own))]
        for i, cols in enumerate(own):
            gather("scalar", late_own[i][:], x_plane[last], slice(parts[3].start + cols.start, parts[3].start + cols.stop))
        for i, cols in enumerate(own):
            move("scalar", grouped[3][:, cols, last], late_own[i][:])

        x_scales = keep.tile([P, S], U8, name="x_scales", align_bytes=64)
        x_codes = []

        def quantise(i):
            cols = parts[i]
            width = cols.stop - cols.start
            tag = ("x_codes0", "shared0", "x_codes2", "x_codes0")[i]
            x_codes.append(keep.tile([P, width], U32, name="x_codes%d" % i, tag=tag, align_bytes=64))
            for lo in range(0, width, QUARTER):
                hi = min(lo + QUARTER, width)
                nc.vector.quantize_mx(
                    out=x_codes[i][:, lo:hi].bitcast(FP8X4),
                    scales=x_scales[:, cols.start + lo : cols.start + hi],
                    in_=grouped[i][:, lo:hi, :].rearrange("p c t -> p (c t)"),
                )

        for i in range(3):
            quantise(i)

        def codes_at(a, n):
            i = max(k for k, cols in enumerate(parts) if cols.start <= a)
            return x_codes[i][:, a - parts[i].start : a - parts[i].start + n]

        def product(m, first, passes):
            rows = slice(m * P, (m + 1) * P)
            acc = psum.tile([P, V], F32, name="acc")
            a = first
            for n in passes:
                nc.tensor.matmul_mx(
                    out=acc[:, a - first : a - first + n],
                    lhsT=w1_codes[:, rows].bitcast(FP8X4),
                    lhsT_scale=s_plane[8:P, rows],
                    rhs=codes_at(a, n).bitcast(FP8X4),
                    rhs_scale=x_scales[:, a : a + n],
                    start=True,
                    stop=True,
                )
                a = a + n
            return acc

        def finish(m, first, width, acc):
            result = keep.tile([P, width], F32, name="result%d_%d" % (first, m))
            nc.vector.tensor_tensor(out=result[:], in0=acc[:, :width], in1=t_picked[:, m, first : first + width], op=ADD)
            nc.sync.dma_start(out=out[m * P : (m + 1) * P, first : first + width], in_=result[:])

        done = [0] * m_tiles
        starts = []
        for m, passes in PIECES:
            starts.append(done[m])
            done[m] = done[m] + sum(passes)
        accs = [product(m, starts[i], passes) for i, (m, passes) in enumerate(PIECES[:2])]
        finish(PIECES[0][0], starts[0], sum(PIECES[0][1]), accs[0])
        quantise(3)
        for i, (m, passes) in enumerate(PIECES):
            if i >= 2:
                accs.append(product(m, starts[i], passes))
            if i >= 1:
                finish(m, starts[i], sum(passes), accs[i])
